import numpy as np
import ml_dtypes


def mxq(x, axis, fmt="e4m3"):
    dtype, down = {"e4m3": (ml_dtypes.float8_e4m3fn, 7), "e5m2": (ml_dtypes.float8_e5m2, 14)}[fmt]
    v = np.moveaxis(np.asarray(x, np.float32).astype(ml_dtypes.bfloat16).astype(np.float64), axis, -1)
    blocks = v.reshape(v.shape[:-1] + (-1, 32))
    amax = np.abs(blocks).max(-1, keepdims=True)
    byte = np.maximum(np.where(amax > 0, np.frexp(amax)[1] - 1 + 127, 0) - down, 1)
    scale = np.exp2(byte - 127.0)
    codes = (blocks / scale).astype(np.float32).astype(dtype).astype(np.float64)
    return np.moveaxis((codes * scale).reshape(v.shape), -1, axis)


WIDE = False


def mx_kscale(k):
    if not WIDE:
        return np.ones(k)
    levels = np.array([10, -10, 5, -5, 0])
    if k % 512:
        return np.exp2(np.random.permutation(np.resize(levels, k // 32))).repeat(32)
    a = np.empty((k // 512, 16))
    for p in range(k // 512):
        a[p, :8] = np.random.permutation(np.resize(levels, 8))
        for g in range(8):
            far = levels[np.abs(levels - a[p, g]) >= 10]
            a[p, g + 8] = far[np.random.randint(len(far))]
    return np.exp2(a.ravel()).repeat(32)


def f64(x):
    return np.asarray(x).astype(np.float64)


def striped8(idx):
    return np.asarray(idx).reshape(8, -1, 16).transpose(0, 2, 1).reshape(128, -1).astype(np.uint16)


def unstriped8(offs):
    return offs.reshape(8, 16, -1).transpose(0, 2, 1).reshape(8, -1).astype(np.int64)


def pick8(x, idx, run):
    r = np.arange(len(x))
    return x[r[:, None], idx[r % (8 * run) // run]]


E2M1 = np.array([0.0, 0.5, 1.0, 1.5, 2.0, 3.0, 4.0, 6.0, -0.0, -0.5, -1.0, -1.5, -2.0, -3.0, -4.0, -6.0])


def pack_weight(w, fmt):
    k, n = w.shape
    w = f64(np.asarray(w, np.float32).astype(ml_dtypes.bfloat16)).reshape(k // 32, 32, n)
    amax = np.abs(w).max(1)
    if fmt == "e4m3":
        byte = np.frexp(amax)[1] - 1 + 127 - 7
    else:
        mant, ex = np.frexp(amax / 6.0)
        byte = np.where(mant > 0.5, ex, ex - 1) + 127
    byte = np.clip(np.where(amax > 0, byte, 1), 1, 254)
    scaled = (w * np.exp2(127.0 - byte)[:, None, :]).reshape(k, n).astype(np.float32)
    by_word = np.ascontiguousarray(scaled.reshape(k // 512, 128, 4, n).transpose(0, 1, 3, 2))
    if fmt == "e4m3":
        words = by_word.astype(ml_dtypes.float8_e4m3fn).view(np.uint8)
    else:
        c = by_word.astype(ml_dtypes.float4_e2m1fn).view(np.uint8) & 0xF
        words = (c[..., 0::2] | (c[..., 1::2] << 4)).reshape(k // 512, 128, 2 * n)
    return np.ascontiguousarray(words), np.ascontiguousarray(byte.astype(np.uint8).reshape(k // 512, 16, n))


def unpack_weight(words, scales, fmt):
    g, _, n = scales.shape
    words = np.ascontiguousarray(words).reshape(g, 128, n, -1)
    if fmt == "e4m3":
        vals = words.view(ml_dtypes.float8_e4m3fn).astype(np.float64)
    else:
        nib = np.empty((g, 128, n, 4), np.uint8)
        nib[..., 0::2] = words & 0xF
        nib[..., 1::2] = words >> 4
        vals = E2M1[nib]
    vals = vals * np.repeat(np.exp2(scales.astype(np.float64) - 127.0), 8, axis=1)[..., None]
    return vals.transpose(0, 1, 3, 2).reshape(g * 512, n)


D, T, U, X, S, I, Q = 512, 1024, 1024, 1024, 1024, 512, 128


def setup_inputs():
    n = np.random.standard_normal
    idx = np.stack([np.random.permutation(U)[:I] for _ in range(8)])
    idx2 = np.stack([np.random.permutation(T)[:I] for _ in range(8)])
    idx3 = np.stack([np.random.permutation(X)[:I] for _ in range(8)])
    idx4 = np.stack([np.random.permutation(T)[:I] for _ in range(8)])
    idx5 = np.stack([np.random.permutation(S)[:I] for _ in range(8)])
    idx6 = np.stack([np.random.permutation(T)[:I] for _ in range(8)])
    idx7 = np.stack([np.random.permutation(T)[:I] for _ in range(8)])
    fd = mx_kscale(D)
    cachep = pack_weight(n((D, T)) / fd[:, None], "e4m3")
    draftp = pack_weight(n((D, U)) / fd[:, None], "e2m1")
    archp = pack_weight(n((D, X)) / fd[:, None], "e4m3")
    prefp = pack_weight(n((D, S)) / fd[:, None], "e2m1")
    return {
        "query": (n((D, Q)) * 1.0 / np.sqrt(D) * fd[:, None]).astype(np.float32),
        "cache_words": cachep[0],
        "cache_scales": cachep[1],
        "draft_words": draftp[0],
        "draft_scales": draftp[1],
        "arch_words": archp[0],
        "arch_scales": archp[1],
        "pref_words": prefp[0],
        "pref_scales": prefp[1],
        "offs": striped8(idx),
        "offs2": striped8(idx2),
        "offs3": striped8(idx3),
        "offs4": striped8(idx4),
        "offs5": striped8(idx5),
        "offs6": striped8(idx6),
        "offs7": striped8(idx7),
    }


def reference(query, cache_words, cache_scales, draft_words, draft_scales, arch_words, arch_scales, pref_words, pref_scales, offs, offs2, offs3, offs4, offs5, offs6, offs7):
    idx = unstriped8(offs)
    idx2 = unstriped8(offs2)
    idx3 = unstriped8(offs3)
    idx4 = unstriped8(offs4)
    idx5 = unstriped8(offs5)
    idx6 = unstriped8(offs6)
    idx7 = unstriped8(offs7)
    cacheu = unpack_weight(cache_words, cache_scales, "e4m3")
    draftu = unpack_weight(draft_words, draft_scales, "e2m1")
    archu = unpack_weight(arch_words, arch_scales, "e4m3")
    prefu = unpack_weight(pref_words, pref_scales, "e2m1")
    queryq = mxq(f64(query), 0, "e4m3")
    a = queryq.T @ cacheu
    b = queryq.T @ draftu
    c0 = queryq.T @ archu
    d0 = queryq.T @ prefu
    f1 = np.zeros((Q, T))
    f1[np.arange(Q)[:, None], idx2[np.arange(Q) % 128 // 16]] = pick8(b, idx, 16)
    f2 = np.zeros((Q, T))
    f2[np.arange(Q)[:, None], idx4[np.arange(Q) % 128 // 16]] = pick8(c0, idx3, 16)
    f3 = np.zeros((Q, T))
    f3[np.arange(Q)[:, None], idx6[np.arange(Q) % 128 // 16]] = pick8(d0, idx5, 16)
    m1 = np.maximum(f1, f2)
    m2 = np.minimum(m1, f3)
    aa = a - m2
    y = pick8(aa, idx7, 16)
    return y

@@ -1,0 +1,159 @@
+from contextlib import ExitStack
+
+import concourse.mybir as mybir
+
+F32 = mybir.dt.float32
+BF16 = mybir.dt.bfloat16
+I32 = mybir.dt.int32
+U32 = mybir.dt.uint32
+U16 = mybir.dt.uint16
+U8 = mybir.dt.uint8
+FP8X4 = mybir.dt.float8_e4m3fn_x4
+FP4X4 = mybir.dt.float4_e2m1fn_x4
+ALU = mybir.AluOpType
+COPY = mybir.ActivationFunctionType.Copy
+
+P = 128
+PACK = 4
+D = 512
+Q = 128
+T = 1024
+SLOTS = 512
+BANK = 512
+LIST_COLS = SLOTS // 16
+FLOPS = 4 * 2 * D * Q * T
+
+
+def tile_attend_fourmeet_four_kernel(
+    tc, query, cache_words, cache_scales, draft_words, draft_scales, arch_words, arch_scales,
+    pref_words, pref_scales, offs, offs2, offs3, offs4, offs5, offs6, offs7, out,
+):
+    nc = tc.nc
+    with ExitStack() as ctx:
+        lists = ctx.enter_context(tc.tile_pool(name="lists", bufs=1))
+        keep = ctx.enter_context(tc.tile_pool(name="keep", bufs=1))
+        psum = ctx.enter_context(tc.psum_pool(name="psum", bufs=1))
+
+        def load_list(name, src):
+            t = lists.tile([P, LIST_COLS], U16, name=name)
+            nc.sync.dma_start(t[:], src)
+            return t
+
+        def zero_plane(name):
+            plane = keep.tile([P, T], U8, name=name, align_bytes=64)
+            nc.vector.memset(plane[:].bitcast(I32), 0)
+            return plane
+
+        def load_scales(plane, scales):
+            for quad in range(4):
+                nc.sync.dma_start(
+                    plane[32 * quad : 32 * quad + 4, :].bitcast(I32),
+                    scales[0, 4 * quad : 4 * quad + 4, :].bitcast(I32),
+                )
+
+        def load_words8(name, words):
+            t = keep.tile([P, 4 * T], U8, name=name, align_bytes=64)
+            nc.sync.dma_start(t[:].bitcast(I32), words[0].rearrange("p n t -> p (n t)").bitcast(I32))
+            return t
+
+        def load_words4(name, words):
+            t = keep.tile([P, 2 * T], U8, name=name, align_bytes=64)
+            nc.sync.dma_start(t[:].bitcast(I32), words[0].bitcast(I32))
+            return t
+
+        def zero_window(name):
+            t = keep.tile([P, T], F32, name=name)
+            nc.vector.memset(t[:], 0.0)
+            return t
+
+        draft_plane = zero_plane("draft_plane")
+        arch_plane = zero_plane("arch_plane")
+        pref_plane = zero_plane("pref_plane")
+        cache_plane = zero_plane("cache_plane")
+        f1 = zero_window("f1")
+        f2 = zero_window("f2")
+        f3 = zero_window("f3")
+
+        q_raw = keep.tile([P, PACK, Q], F32, name="q_raw")
+        nc.sync.dma_start(q_raw[:], query.rearrange("(p j) q -> p j q", j=PACK))
+        load_scales(draft_plane, draft_scales)
+        draft_codes = load_words4("draft_codes", draft_words)
+        o1 = load_list("o1", offs)
+        o2 = load_list("o2", offs2)
+        load_scales(arch_plane, arch_scales)
+        arch_codes = load_words8("arch_codes", arch_words)
+        o3 = load_list("o3", offs3)
+        o4 = load_list("o4", offs4)
+        load_scales(pref_plane, pref_scales)
+        pref_codes = load_words4("pref_codes", pref_words)
+        o5 = load_list("o5", offs5)
+        o6 = load_list("o6", offs6)
+        load_scales(cache_plane, cache_scales)
+        cache_codes = load_words8("cache_codes", cache_words)
+        o7 = load_list("o7", offs7)
+
+        q_grouped = keep.tile([P, Q, PACK], BF16, name="q_grouped", align_bytes=64)
+        nc.vector.tensor_copy(out=q_grouped[:], in_=q_raw[:].rearrange("p j q -> p q j"))
+        q_codes = keep.tile([P, Q], U32, name="q_codes", align_bytes=64)
+        q_plane = keep.tile([P, Q], U8, name="q_plane", align_bytes=64)
+        nc.vector.quantize_mx(
+            out=q_codes[:].bitcast(FP8X4), scales=q_plane[:], in_=q_grouped[:].rearrange("p q j -> p (q j)")
+        )
+
+        def score(bank, codes, width, dtype, plane, c0, n):
+            acc = psum.tile([Q, n], F32, name="acc", tag="bank%d" % bank)
+            nc.tensor.matmul_mx(
+                out=acc[:],
+                lhsT=q_codes[:].bitcast(FP8X4),
+                lhsT_scale=q_plane[:],
+                rhs=codes[:, width * c0 : width * (c0 + n)].bitcast(dtype),
+                rhs_scale=plane[:, c0 : c0 + n],
+                start=True,
+                stop=True,
+            )
+            return acc
+
+        half = LIST_COLS // 2
+
+        b = keep.tile([Q, T], F32, name="b")
+        for j in range(4):
+            acc = score(j, draft_codes, 2, FP4X4, draft_plane, 256 * j, 256)
+            if j % 2 == 0:
+                nc.scalar.activation(b[:, 256 * j : 256 * (j + 1)], acc[:], COPY)
+            else:
+                nc.vector.tensor_copy(b[:, 256 * j : 256 * (j + 1)], acc[:])
+        for h in range(2):
+            gb = keep.tile([Q, SLOTS // 2], F32, name="gb%d" % h)
+            nc.vector.tensor_copy(gb[:], b[:].indirect(o1[:, h * half : (h + 1) * half]))
+            nc.scalar.activation(f1[:].indirect(o2[:, h * half : (h + 1) * half]), gb[:], COPY)
+
+        def put(name, first_bank, codes, width, dtype, plane, take, place, window):
+            s = keep.tile([Q, T], F32, name=name)
+            for j in range(2):
+                acc = score(first_bank + j, codes, width, dtype, plane, BANK * j, BANK)
+                nc.vector.tensor_copy(s[:, BANK * j : BANK * (j + 1)], acc[:])
+            g = keep.tile([Q, SLOTS], F32, name="g" + name)
+            nc.vector.tensor_copy(g[:], s[:].indirect(take[:]))
+            nc.scalar.activation(window[:].indirect(place[:]), g[:], COPY)
+
+        put("c0", 0, arch_codes, 4, FP8X4, arch_plane, o3, o4, f2)
+        put("d0", 2, pref_codes, 2, FP4X4, pref_plane, o5, o6, f3)
+
+        a_banks = [score(4 + j, cache_codes, 4, FP8X4, cache_plane, BANK * j, BANK) for j in range(2)]
+        m1 = keep.tile([Q, T], F32, name="m1")
+        nc.vector.tensor_tensor(m1[:], f1[:], f2[:], ALU.max)
+        m2 = keep.tile([Q, T], F32, name="m2")
+        aa = keep.tile([Q, T], F32, name="aa")
+        for j in range(2):
+            cols = slice(BANK * j, BANK * (j + 1))
+            nc.vector.tensor_tensor(m2[:, cols], m1[:, cols], f3[:, cols], ALU.min)
+        for j in range(2):
+            cols = slice(BANK * j, BANK * (j + 1))
+            nc.vector.tensor_tensor(aa[:, cols], a_banks[j][:], m2[:, cols], ALU.subtract)
+
+        y0 = keep.tile([Q, SLOTS // 2], F32, name="y0")
+        y1 = keep.tile([Q, SLOTS // 2], F32, name="y1")
+        nc.vector.tensor_copy(y0[:], aa[:].indirect(o7[:, 0:half]))
+        nc.scalar.activation(y1[:], aa[:].indirect(o7[:, half:LIST_COLS]), COPY)
+        nc.sync.dma_start(out[:, 0 : SLOTS // 2], y0[:])
+        nc.scalar.dma_start(out[:, SLOTS // 2 : SLOTS], y1[:])

@@ -57,7 +57,7 @@ def tile_attend_fourmeet_four_kernel(
             return t
 
         def load_words4(name, words):
-            t = keep.tile([P, 2 * T], U8, name=name, align_bytes=64)
+            t = keep.tile([P, 2 * T], U8, name=name, tag=name, align_bytes=64)
             nc.sync.dma_start(t[:].bitcast(I32), words[0].bitcast(I32))
             return t
 
@@ -71,8 +71,6 @@ def tile_attend_fourmeet_four_kernel(
         pref_plane = zero_plane("pref_plane")
         cache_plane = zero_plane("cache_plane")
         f1 = zero_window("f1")
-        f2 = zero_window("f2")
-        f3 = zero_window("f3")
 
         q_raw = keep.tile([P, PACK, Q], F32, name="q_raw")
         nc.sync.dma_start(q_raw[:], query.rearrange("(p j) q -> p j q", j=PACK))
@@ -92,7 +90,7 @@ def tile_attend_fourmeet_four_kernel(
         cache_codes = load_words8("cache_codes", cache_words)
         o7 = load_list("o7", offs7)
 
-        q_grouped = keep.tile([P, Q, PACK], BF16, name="q_grouped", align_bytes=64)
+        q_grouped = keep.tile([P, Q, PACK], BF16, name="q_grouped", tag="q_grouped", align_bytes=64)
         nc.vector.tensor_copy(out=q_grouped[:], in_=q_raw[:].rearrange("p j q -> p q j"))
         q_codes = keep.tile([P, Q], U32, name="q_codes", align_bytes=64)
         q_plane = keep.tile([P, Q], U8, name="q_plane", align_bytes=64)
@@ -114,6 +112,8 @@ def tile_attend_fourmeet_four_kernel(
             return acc
 
         half = LIST_COLS // 2
+        f2 = keep.tile([P, T], F32, name="f2", tag="q_grouped", align_bytes=64)
+        nc.gpsimd.memset(f2[:], 0.0)
 
         b = keep.tile([Q, T], F32, name="b")
         for j in range(4):
@@ -122,25 +122,27 @@ def tile_attend_fourmeet_four_kernel(
                 nc.scalar.activation(b[:, 256 * j : 256 * (j + 1)], acc[:], COPY)
             else:
                 nc.vector.tensor_copy(b[:, 256 * j : 256 * (j + 1)], acc[:])
+        f3 = keep.tile([P, T], F32, name="f3", tag="draft_codes", align_bytes=64)
+        nc.gpsimd.memset(f3[:], 0.0)
         for h in range(2):
             gb = keep.tile([Q, SLOTS // 2], F32, name="gb%d" % h)
             nc.vector.tensor_copy(gb[:], b[:].indirect(o1[:, h * half : (h + 1) * half]))
             nc.scalar.activation(f1[:].indirect(o2[:, h * half : (h + 1) * half]), gb[:], COPY)
 
         def put(name, first_bank, codes, width, dtype, plane, take, place, window):
-            s = keep.tile([Q, T], F32, name=name)
+            s = keep.tile([Q, T], F32, name=name, tag=name)
             for j in range(2):
-                acc = score(first_bank + j, codes, width, dtype, plane, BANK * j, BANK)
+                acc = score(first_bank - j, codes, width, dtype, plane, BANK * j, BANK)
                 nc.vector.tensor_copy(s[:, BANK * j : BANK * (j + 1)], acc[:])
             g = keep.tile([Q, SLOTS], F32, name="g" + name)
             nc.vector.tensor_copy(g[:], s[:].indirect(take[:]))
             nc.scalar.activation(window[:].indirect(place[:]), g[:], COPY)
 
-        put("c0", 0, arch_codes, 4, FP8X4, arch_plane, o3, o4, f2)
-        put("d0", 2, pref_codes, 2, FP4X4, pref_plane, o5, o6, f3)
+        put("c0", 3, arch_codes, 4, FP8X4, arch_plane, o3, o4, f2)
+        put("d0", 3, pref_codes, 2, FP4X4, pref_plane, o5, o6, f3)
 
         a_banks = [score(4 + j, cache_codes, 4, FP8X4, cache_plane, BANK * j, BANK) for j in range(2)]
-        m1 = keep.tile([Q, T], F32, name="m1")
+        m1 = keep.tile([Q, T], F32, name="m1", tag="d0")
         nc.vector.tensor_tensor(m1[:], f1[:], f2[:], ALU.max)
         m2 = keep.tile([Q, T], F32, name="m2")
         aa = keep.tile([Q, T], F32, name="aa")

@@ -61,16 +61,12 @@ def tile_attend_fourmeet_four_kernel(
             nc.sync.dma_start(t[:].bitcast(I32), words[0].bitcast(I32))
             return t
 
-        def zero_window(name):
-            t = keep.tile([P, T], F32, name=name)
-            nc.vector.memset(t[:], 0.0)
-            return t
-
-        draft_plane = zero_plane("draft_plane")
+        draft_plane = keep.tile([P, T], U8, name="draft_plane", align_bytes=64)
+        nc.vector.memset(draft_plane[:, 0 : T // 2].bitcast(I32), 0)
+        nc.gpsimd.memset(draft_plane[:, T // 2 : T].bitcast(I32), 0)
         arch_plane = zero_plane("arch_plane")
         pref_plane = zero_plane("pref_plane")
         cache_plane = zero_plane("cache_plane")
-        f1 = zero_window("f1")
 
         q_raw = keep.tile([P, PACK, Q], F32, name="q_raw")
         nc.sync.dma_start(q_raw[:], query.rearrange("(p j) q -> p j q", j=PACK))
@@ -78,10 +74,10 @@ def tile_attend_fourmeet_four_kernel(
         draft_codes = load_words4("draft_codes", draft_words)
         o1 = load_list("o1", offs)
         o2 = load_list("o2", offs2)
-        load_scales(arch_plane, arch_scales)
-        arch_codes = load_words8("arch_codes", arch_words)
         o3 = load_list("o3", offs3)
         o4 = load_list("o4", offs4)
+        arch_codes = load_words8("arch_codes", arch_words)
+        load_scales(arch_plane, arch_scales)
         load_scales(pref_plane, pref_scales)
         pref_codes = load_words4("pref_codes", pref_words)
         o5 = load_list("o5", offs5)
@@ -112,22 +108,24 @@ def tile_attend_fourmeet_four_kernel(
             return acc
 
         half = LIST_COLS // 2
-        f2 = keep.tile([P, T], F32, name="f2", tag="q_grouped", align_bytes=64)
-        nc.gpsimd.memset(f2[:], 0.0)
+        f1 = keep.tile([P, T], F32, name="f1", tag="q_grouped", align_bytes=64)
+        nc.gpsimd.memset(f1[:], 0.0)
 
-        b = keep.tile([Q, T], F32, name="b")
-        for j in range(4):
-            acc = score(j, draft_codes, 2, FP4X4, draft_plane, 256 * j, 256)
+        b = keep.tile([Q, T], F32, name="b", tag="b")
+        c0 = 0
+        for j, n in enumerate((256, 256, 256, 256)):
+            acc = score(j, draft_codes, 2, FP4X4, draft_plane, c0, n)
             if j % 2 == 0:
-                nc.scalar.activation(b[:, 256 * j : 256 * (j + 1)], acc[:], COPY)
+                nc.scalar.activation(b[:, c0 : c0 + n], acc[:], COPY)
             else:
-                nc.vector.tensor_copy(b[:, 256 * j : 256 * (j + 1)], acc[:])
-        f3 = keep.tile([P, T], F32, name="f3", tag="draft_codes", align_bytes=64)
-        nc.gpsimd.memset(f3[:], 0.0)
-        for h in range(2):
-            gb = keep.tile([Q, SLOTS // 2], F32, name="gb%d" % h)
-            nc.vector.tensor_copy(gb[:], b[:].indirect(o1[:, h * half : (h + 1) * half]))
-            nc.scalar.activation(f1[:].indirect(o2[:, h * half : (h + 1) * half]), gb[:], COPY)
+                nc.vector.tensor_copy(b[:, c0 : c0 + n], acc[:])
+            c0 = c0 + n
+        gb = keep.tile([Q, SLOTS], F32, name="gb")
+        nc.scalar.activation(gb[:, 0 : SLOTS // 2], b[:].indirect(o1[:, 0:half]), COPY)
+        nc.vector.tensor_copy(gb[:, SLOTS // 2 : SLOTS], b[:].indirect(o1[:, half:LIST_COLS]))
+        nc.scalar.activation(f1[:].indirect(o2[:]), gb[:], COPY)
+        f2 = keep.tile([P, T], F32, name="f2", tag="b")
+        nc.gpsimd.memset(f2[:], 0.0)
 
         def put(name, first_bank, codes, width, dtype, plane, take, place, window):
             s = keep.tile([Q, T], F32, name=name, tag=name)
@@ -139,19 +137,29 @@ def tile_attend_fourmeet_four_kernel(
             nc.scalar.activation(window[:].indirect(place[:]), g[:], COPY)
 
         put("c0", 3, arch_codes, 4, FP8X4, arch_plane, o3, o4, f2)
+        f3 = keep.tile([P, T], F32, name="f3", tag="c0")
+        nc.gpsimd.memset(f3[:], 0.0)
         put("d0", 3, pref_codes, 2, FP4X4, pref_plane, o5, o6, f3)
 
         a_banks = [score(4 + j, cache_codes, 4, FP8X4, cache_plane, BANK * j, BANK) for j in range(2)]
+        split = T - 256
+        a_tail = keep.tile([Q, T - split], F32, name="a_tail")
+        nc.vector.tensor_copy(a_tail[:], a_banks[1][:, split - BANK : BANK])
         m1 = keep.tile([Q, T], F32, name="m1", tag="d0")
         nc.vector.tensor_tensor(m1[:], f1[:], f2[:], ALU.max)
-        m2 = keep.tile([Q, T], F32, name="m2")
+        u = keep.tile([Q, T], F32, name="u")
+        for j in range(2):
+            cols = slice(BANK * j, BANK * (j + 1))
+            nc.vector.tensor_tensor(u[:, cols], a_banks[j][:], m1[:, cols], ALU.subtract)
+        w = keep.tile([Q, split], F32, name="w")
+        w_tail = keep.tile([Q, T - split], F32, name="w_tail")
         aa = keep.tile([Q, T], F32, name="aa")
-        for j in range(2):
-            cols = slice(BANK * j, BANK * (j + 1))
-            nc.vector.tensor_tensor(m2[:, cols], m1[:, cols], f3[:, cols], ALU.min)
-        for j in range(2):
-            cols = slice(BANK * j, BANK * (j + 1))
-            nc.vector.tensor_tensor(aa[:, cols], a_banks[j][:], m2[:, cols], ALU.subtract)
+        nc.gpsimd.tensor_tensor(w_tail[:], a_tail[:], f3[:, split:T], ALU.subtract)
+        nc.vector.tensor_tensor(w[:, 0:BANK], a_banks[0][:], f3[:, 0:BANK], ALU.subtract)
+        nc.vector.tensor_tensor(w[:, BANK:split], a_banks[1][:, 0 : split - BANK], f3[:, BANK:split], ALU.subtract)
+        nc.vector.tensor_tensor(aa[:, 0:BANK], u[:, 0:BANK], w[:, 0:BANK], ALU.max)
+        nc.vector.tensor_tensor(aa[:, BANK:split], u[:, BANK:split], w[:, BANK:split], ALU.max)
+        nc.vector.tensor_tensor(aa[:, split:T], u[:, split:T], w_tail[:], ALU.max)
 
         y0 = keep.tile([Q, SLOTS // 2], F32, name="y0")
         y1 = keep.tile([Q, SLOTS // 2], F32, name="y1")

@@ -87,7 +87,9 @@ def tile_attend_fourmeet_four_kernel(
         o7 = load_list("o7", offs7)
 
         q_grouped = keep.tile([P, Q, PACK], BF16, name="q_grouped", tag="q_grouped", align_bytes=64)
-        nc.vector.tensor_copy(out=q_grouped[:], in_=q_raw[:].rearrange("p j q -> p q j"))
+        q_by_row = q_raw[:].rearrange("p j q -> p q j")
+        nc.vector.tensor_copy(out=q_grouped[:, 0:80, :], in_=q_by_row[:, 0:80, :])
+        nc.scalar.activation(q_grouped[:, 80:Q, :], q_by_row[:, 80:Q, :], COPY)
         q_codes = keep.tile([P, Q], U32, name="q_codes", align_bytes=64)
         q_plane = keep.tile([P, Q], U8, name="q_plane", align_bytes=64)
         nc.vector.quantize_mx(
@@ -113,7 +115,7 @@ def tile_attend_fourmeet_four_kernel(
 
         b = keep.tile([Q, T], F32, name="b", tag="b")
         c0 = 0
-        for j, n in enumerate((256, 256, 256, 256)):
+        for j, n in enumerate((256, 256, 128, 128, 128, 128)):
             acc = score(j, draft_codes, 2, FP4X4, draft_plane, c0, n)
             if j % 2 == 0:
                 nc.scalar.activation(b[:, c0 : c0 + n], acc[:], COPY)
@@ -136,12 +138,12 @@ def tile_attend_fourmeet_four_kernel(
             nc.vector.tensor_copy(g[:], s[:].indirect(take[:]))
             nc.scalar.activation(window[:].indirect(place[:]), g[:], COPY)
 
-        put("c0", 3, arch_codes, 4, FP8X4, arch_plane, o3, o4, f2)
+        put("c0", 5, arch_codes, 4, FP8X4, arch_plane, o3, o4, f2)
         f3 = keep.tile([P, T], F32, name="f3", tag="c0")
         nc.gpsimd.memset(f3[:], 0.0)
-        put("d0", 3, pref_codes, 2, FP4X4, pref_plane, o5, o6, f3)
+        put("d0", 5, pref_codes, 2, FP4X4, pref_plane, o5, o6, f3)
 
-        a_banks = [score(4 + j, cache_codes, 4, FP8X4, cache_plane, BANK * j, BANK) for j in range(2)]
+        a_banks = [score(6 + j, cache_codes, 4, FP8X4, cache_plane, BANK * j, BANK) for j in range(2)]
         split = T - 256
         a_tail = keep.tile([Q, T - split], F32, name="a_tail")
         nc.vector.tensor_copy(a_tail[:], a_banks[1][:, split - BANK : BANK])

@@ -74,10 +74,10 @@ def tile_attend_fourmeet_four_kernel(
         draft_codes = load_words4("draft_codes", draft_words)
         o1 = load_list("o1", offs)
         o2 = load_list("o2", offs2)
+        load_scales(arch_plane, arch_scales)
+        arch_codes = load_words8("arch_codes", arch_words)
         o3 = load_list("o3", offs3)
         o4 = load_list("o4", offs4)
-        arch_codes = load_words8("arch_codes", arch_words)
-        load_scales(arch_plane, arch_scales)
         load_scales(pref_plane, pref_scales)
         pref_codes = load_words4("pref_codes", pref_words)
         o5 = load_list("o5", offs5)

from contextlib import ExitStack

import concourse.mybir as mybir

F32 = mybir.dt.float32
BF16 = mybir.dt.bfloat16
I32 = mybir.dt.int32
U32 = mybir.dt.uint32
U16 = mybir.dt.uint16
U8 = mybir.dt.uint8
FP8X4 = mybir.dt.float8_e4m3fn_x4
FP4X4 = mybir.dt.float4_e2m1fn_x4
ALU = mybir.AluOpType
COPY = mybir.ActivationFunctionType.Copy

P = 128
PACK = 4
D = 512
Q = 128
T = 1024
SLOTS = 512
BANK = 512
LIST_COLS = SLOTS // 16
FLOPS = 4 * 2 * D * Q * T


def tile_attend_fourmeet_four_kernel(
    tc, query, cache_words, cache_scales, draft_words, draft_scales, arch_words, arch_scales,
    pref_words, pref_scales, offs, offs2, offs3, offs4, offs5, offs6, offs7, out,
):
    nc = tc.nc
    with ExitStack() as ctx:
        lists = ctx.enter_context(tc.tile_pool(name="lists", bufs=1))
        keep = ctx.enter_context(tc.tile_pool(name="keep", bufs=1))
        psum = ctx.enter_context(tc.psum_pool(name="psum", bufs=1))

        def load_list(name, src):
            t = lists.tile([P, LIST_COLS], U16, name=name)
            nc.sync.dma_start(t[:], src)
            return t

        def zero_plane(name):
            plane = keep.tile([P, T], U8, name=name, align_bytes=64)
            nc.vector.memset(plane[:].bitcast(I32), 0)
            return plane

        def load_scales(plane, scales):
            for quad in range(4):
                nc.sync.dma_start(
                    plane[32 * quad : 32 * quad + 4, :].bitcast(I32),
                    scales[0, 4 * quad : 4 * quad + 4, :].bitcast(I32),
                )

        def load_words8(name, words):
            t = keep.tile([P, 4 * T], U8, name=name, align_bytes=64)
            nc.sync.dma_start(t[:].bitcast(I32), words[0].rearrange("p n t -> p (n t)").bitcast(I32))
            return t

        def load_words4(name, words):
            t = keep.tile([P, 2 * T], U8, name=name, tag=name, align_bytes=64)
            nc.sync.dma_start(t[:].bitcast(I32), words[0].bitcast(I32))
            return t

        draft_plane = keep.tile([P, T], U8, name="draft_plane", align_bytes=64)
        nc.vector.memset(draft_plane[:, 0 : T // 2].bitcast(I32), 0)
        nc.gpsimd.memset(draft_plane[:, T // 2 : T].bitcast(I32), 0)
        arch_plane = zero_plane("arch_plane")
        pref_plane = zero_plane("pref_plane")
        cache_plane = zero_plane("cache_plane")

        q_raw = keep.tile([P, PACK, Q], F32, name="q_raw")
        nc.sync.dma_start(q_raw[:], query.rearrange("(p j) q -> p j q", j=PACK))
        load_scales(draft_plane, draft_scales)
        draft_codes = load_words4("draft_codes", draft_words)
        o1 = load_list("o1", offs)
        o2 = load_list("o2", offs2)
        load_scales(arch_plane, arch_scales)
        arch_codes = load_words8("arch_codes", arch_words)
        o3 = load_list("o3", offs3)
        o4 = load_list("o4", offs4)
        load_scales(pref_plane, pref_scales)
        pref_codes = load_words4("pref_codes", pref_words)
        o5 = load_list("o5", offs5)
        o6 = load_list("o6", offs6)
        load_scales(cache_plane, cache_scales)
        cache_codes = load_words8("cache_codes", cache_words)
        o7 = load_list("o7", offs7)

        q_grouped = keep.tile([P, Q, PACK], BF16, name="q_grouped", tag="q_grouped", align_bytes=64)
        q_by_row = q_raw[:].rearrange("p j q -> p q j")
        nc.vector.tensor_copy(out=q_grouped[:, 0:80, :], in_=q_by_row[:, 0:80, :])
        nc.scalar.activation(q_grouped[:, 80:Q, :], q_by_row[:, 80:Q, :], COPY)
        q_codes = keep.tile([P, Q], U32, name="q_codes", align_bytes=64)
        q_plane = keep.tile([P, Q], U8, name="q_plane", align_bytes=64)
        nc.vector.quantize_mx(
            out=q_codes[:].bitcast(FP8X4), scales=q_plane[:], in_=q_grouped[:].rearrange("p q j -> p (q j)")
        )

        def score(bank, codes, width, dtype, plane, c0, n):
            acc = psum.tile([Q, n], F32, name="acc", tag="bank%d" % bank)
            nc.tensor.matmul_mx(
                out=acc[:],
                lhsT=q_codes[:].bitcast(FP8X4),
                lhsT_scale=q_plane[:],
                rhs=codes[:, width * c0 : width * (c0 + n)].bitcast(dtype),
                rhs_scale=plane[:, c0 : c0 + n],
                start=True,
                stop=True,
            )
            return acc

        half = LIST_COLS // 2
        f1 = keep.tile([P, T], F32, name="f1", tag="q_grouped", align_bytes=64)
        nc.gpsimd.memset(f1[:], 0.0)

        b = keep.tile([Q, T], F32, name="b", tag="b")
        c0 = 0
        for j, n in enumerate((256, 256, 128, 128, 128, 128)):
            acc = score(j, draft_codes, 2, FP4X4, draft_plane, c0, n)
            if j % 2 == 0:
                nc.scalar.activation(b[:, c0 : c0 + n], acc[:], COPY)
            else:
                nc.vector.tensor_copy(b[:, c0 : c0 + n], acc[:])
            c0 = c0 + n
        gb = keep.tile([Q, SLOTS], F32, name="gb")
        nc.scalar.activation(gb[:, 0 : SLOTS // 2], b[:].indirect(o1[:, 0:half]), COPY)
        nc.vector.tensor_copy(gb[:, SLOTS // 2 : SLOTS], b[:].indirect(o1[:, half:LIST_COLS]))
        nc.scalar.activation(f1[:].indirect(o2[:]), gb[:], COPY)
        f2 = keep.tile([P, T], F32, name="f2", tag="b")
        nc.gpsimd.memset(f2[:], 0.0)

        def put(name, first_bank, codes, width, dtype, plane, take, place, window):
            s = keep.tile([Q, T], F32, name=name, tag=name)
            for j in range(2):
                acc = score(first_bank - j, codes, width, dtype, plane, BANK * j, BANK)
                nc.vector.tensor_copy(s[:, BANK * j : BANK * (j + 1)], acc[:])
            g = keep.tile([Q, SLOTS], F32, name="g" + name)
            nc.vector.tensor_copy(g[:], s[:].indirect(take[:]))
            nc.scalar.activation(window[:].indirect(place[:]), g[:], COPY)

        put("c0", 5, arch_codes, 4, FP8X4, arch_plane, o3, o4, f2)
        f3 = keep.tile([P, T], F32, name="f3", tag="c0")
        nc.gpsimd.memset(f3[:], 0.0)
        put("d0", 5, pref_codes, 2, FP4X4, pref_plane, o5, o6, f3)

        a_banks = [score(6 + j, cache_codes, 4, FP8X4, cache_plane, BANK * j, BANK) for j in range(2)]
        split = T - 256
        a_tail = keep.tile([Q, T - split], F32, name="a_tail")
        nc.vector.tensor_copy(a_tail[:], a_banks[1][:, split - BANK : BANK])
        m1 = keep.tile([Q, T], F32, name="m1", tag="d0")
        nc.vector.tensor_tensor(m1[:], f1[:], f2[:], ALU.max)
        u = keep.tile([Q, T], F32, name="u")
        for j in range(2):
            cols = slice(BANK * j, BANK * (j + 1))
            nc.vector.tensor_tensor(u[:, cols], a_banks[j][:], m1[:, cols], ALU.subtract)
        w = keep.tile([Q, split], F32, name="w")
        w_tail = keep.tile([Q, T - split], F32, name="w_tail")
        aa = keep.tile([Q, T], F32, name="aa")
        nc.gpsimd.tensor_tensor(w_tail[:], a_tail[:], f3[:, split:T], ALU.subtract)
        nc.vector.tensor_tensor(w[:, 0:BANK], a_banks[0][:], f3[:, 0:BANK], ALU.subtract)
        nc.vector.tensor_tensor(w[:, BANK:split], a_banks[1][:, 0 : split - BANK], f3[:, BANK:split], ALU.subtract)
        nc.vector.tensor_tensor(aa[:, 0:BANK], u[:, 0:BANK], w[:, 0:BANK], ALU.max)
        nc.vector.tensor_tensor(aa[:, BANK:split], u[:, BANK:split], w[:, BANK:split], ALU.max)
        nc.vector.tensor_tensor(aa[:, split:T], u[:, split:T], w_tail[:], ALU.max)

        y0 = keep.tile([Q, SLOTS // 2], F32, name="y0")
        y1 = keep.tile([Q, SLOTS // 2], F32, name="y1")
        nc.vector.tensor_copy(y0[:], aa[:].indirect(o7[:, 0:half]))
        nc.scalar.activation(y1[:], aa[:].indirect(o7[:, half:LIST_COLS]), COPY)
        nc.sync.dma_start(out[:, 0 : SLOTS // 2], y0[:])
        nc.scalar.dma_start(out[:, SLOTS // 2 : SLOTS], y1[:])
